import numpy as np
import ml_dtypes


def mxq(x, axis, fmt="e4m3"):
    dtype, down = {"e4m3": (ml_dtypes.float8_e4m3fn, 7), "e5m2": (ml_dtypes.float8_e5m2, 14)}[fmt]
    v = np.moveaxis(np.asarray(x, np.float32).astype(ml_dtypes.bfloat16).astype(np.float64), axis, -1)
    blocks = v.reshape(v.shape[:-1] + (-1, 32))
    amax = np.abs(blocks).max(-1, keepdims=True)
    byte = np.maximum(np.where(amax > 0, np.frexp(amax)[1] - 1 + 127, 0) - down, 1)
    scale = np.exp2(byte - 127.0)
    codes = (blocks / scale).astype(np.float32).astype(dtype).astype(np.float64)
    return np.moveaxis((codes * scale).reshape(v.shape), -1, axis)


WIDE = False


def mx_kscale(k):
    if not WIDE:
        return np.ones(k)
    levels = np.array([10, -10, 5, -5, 0])
    if k % 512:
        return np.exp2(np.random.permutation(np.resize(levels, k // 32))).repeat(32)
    a = np.empty((k // 512, 16))
    for p in range(k // 512):
        a[p, :8] = np.random.permutation(np.resize(levels, 8))
        for g in range(8):
            far = levels[np.abs(levels - a[p, g]) >= 10]
            a[p, g + 8] = far[np.random.randint(len(far))]
    return np.exp2(a.ravel()).repeat(32)


def f64(x):
    return np.asarray(x).astype(np.float64)


def striped(idx):
    return np.tile(idx.reshape(-1, 16).T, (8, 1)).astype(np.uint16)


def unstriped(offs):
    return offs[:16].T.reshape(-1).astype(np.int64)


E2M1 = np.array([0.0, 0.5, 1.0, 1.5, 2.0, 3.0, 4.0, 6.0, -0.0, -0.5, -1.0, -1.5, -2.0, -3.0, -4.0, -6.0])


def pack_weight(w, fmt):
    k, n = w.shape
    w = f64(np.asarray(w, np.float32).astype(ml_dtypes.bfloat16)).reshape(k // 32, 32, n)
    amax = np.abs(w).max(1)
    if fmt == "e4m3":
        byte = np.frexp(amax)[1] - 1 + 127 - 7
    else:
        mant, ex = np.frexp(amax / 6.0)
        byte = np.where(mant > 0.5, ex, ex - 1) + 127
    byte = np.clip(np.where(amax > 0, byte, 1), 1, 254)
    scaled = (w * np.exp2(127.0 - byte)[:, None, :]).reshape(k, n).astype(np.float32)
    by_word = np.ascontiguousarray(scaled.reshape(k // 512, 128, 4, n).transpose(0, 1, 3, 2))
    if fmt == "e4m3":
        words = by_word.astype(ml_dtypes.float8_e4m3fn).view(np.uint8)
    else:
        c = by_word.astype(ml_dtypes.float4_e2m1fn).view(np.uint8) & 0xF
        words = (c[..., 0::2] | (c[..., 1::2] << 4)).reshape(k // 512, 128, 2 * n)
    return np.ascontiguousarray(words), np.ascontiguousarray(byte.astype(np.uint8).reshape(k // 512, 16, n))


def unpack_weight(words, scales, fmt):
    g, _, n = scales.shape
    words = np.ascontiguousarray(words).reshape(g, 128, n, -1)
    if fmt == "e4m3":
        vals = words.view(ml_dtypes.float8_e4m3fn).astype(np.float64)
    else:
        nib = np.empty((g, 128, n, 4), np.uint8)
        nib[..., 0::2] = words & 0xF
        nib[..., 1::2] = words >> 4
        vals = E2M1[nib]
    vals = vals * np.repeat(np.exp2(scales.astype(np.float64) - 127.0), 8, axis=1)[..., None]
    return vals.transpose(0, 1, 3, 2).reshape(g * 512, n)


def relu(v):
    return np.maximum(v, 0.0)


K, T, E, C, N = 1536, 512, 12, 128, 128
TOP = 3


def by_expert(wq, xq):
    return np.concatenate([wq[e].T @ xq[:, e * C:(e + 1) * C] for e in range(E)], axis=1)


def setup_inputs():
    n = np.random.standard_normal
    s = mx_kscale(K)[:, None]
    deal = np.repeat(np.arange(E), C).reshape(TOP, T)[:, np.random.permutation(T)]
    deal = np.take_along_axis(deal, np.argsort(np.random.rand(TOP, T), axis=0), axis=0)
    for _ in range(8):
        s_, t_ = np.random.permutation(T).reshape(2, -1); r = np.random.randint(TOP, size=T // 2); x, y = deal[r, s_].copy(), deal[r, t_].copy()
        ok = ~((deal[:, s_] == y).any(0) | (deal[:, t_] == x).any(0)); deal[r[ok], s_[ok]] = y[ok]; deal[r[ok], t_[ok]] = x[ok]
    order = np.lexsort((np.random.rand(TOP * T), deal.reshape(-1)))
    slot_token = order % T; pos = np.empty(TOP * T, np.int64); pos[order] = np.arange(TOP * T); pos = pos.reshape(TOP, T)
    g = np.random.uniform(0.5, 1.5, (TOP, T)); g = g / g.sum(0)
    w = [pack_weight(m, "e2m1") for m in n((E + 1, K, N)) / np.sqrt(K) / s[None]]
    return {
        "xT": (n((K, T)) * s).astype(np.float32),
        "w_words": np.stack([m[0] for m in w]),
        "w_scales": np.stack([m[1] for m in w]),
        "b": (0.3 * n((N, E + 1))).astype(np.float32),
        "gate": np.stack([np.tile(r, (N, 1)) for r in g]).astype(np.float32),
        "offs": striped(slot_token),
        "pos1": striped(pos[0]),
        "pos2": striped(pos[1]),
        "pos3": striped(pos[2]),
    }


def reference(xT, w_words, w_scales, b, gate, offs, pos1, pos2, pos3):
    idx = unstriped(offs)
    w = np.stack([unpack_weight(w_words[e], w_scales[e], "e2m1") for e in range(E + 1)])
    wq = w
    xs = mxq(f64(xT), 0, "e4m3")
    ys = relu((wq[E].T @ xs) + f64(b)[:, E:])
    xq = mxq(f64(xT)[:, idx], 0, "e4m3")
    y = by_expert(w, xq)
    y = relu(y + np.repeat(f64(b)[:, :E], C, axis=1))
    return ys + sum(f64(gate[r]) * y[:, unstriped(p)] for r, p in enumerate((pos1, pos2, pos3)))

@@ -1,0 +1,176 @@
+from contextlib import ExitStack
+
+import concourse.mybir as mybir
+
+K, T, E, C, N = 1536, 512, 12, 128, 128
+TOP = 3
+S = E * C
+FLOPS = 2 * K * N * (S + T)
+
+F32 = mybir.dt.float32
+BF16 = mybir.dt.bfloat16
+I32 = mybir.dt.int32
+U32 = mybir.dt.uint32
+U16 = mybir.dt.uint16
+U8 = mybir.dt.uint8
+FP8X4 = mybir.dt.float8_e4m3fn_x4
+FP4X4 = mybir.dt.float4_e2m1fn_x4
+RELU = mybir.ActivationFunctionType.Relu
+MULT = mybir.AluOpType.mult
+ADD = mybir.AluOpType.add
+
+P = 128
+PASSES = K // 512
+CH = 512
+CHUNKS = S // CH
+PAD = 1536
+
+
+def tile_moe_shr_lin_relu_kernel(
+    tc, xT, w_words, w_scales, b, gate, offs, pos1, pos2, pos3, out
+):
+    nc = tc.nc
+    with ExitStack() as ctx:
+        lists = ctx.enter_context(tc.tile_pool(name="lists", bufs=1))
+        keep = ctx.enter_context(tc.tile_pool(name="keep", bufs=1))
+        psum = ctx.enter_context(tc.psum_pool(name="psum", bufs=1))
+
+        planes = keep.tile([P, 2 * (2 * PASSES * T + PAD)], BF16, name="planes", align_bytes=64)
+        plane_words = planes[:].bitcast(U32)
+        w_sc = keep.tile([P, (E + 1) * PASSES, N], U8, name="w_sc", align_bytes=64)
+        w_cd = keep.tile([P, (E + 1) * PASSES, 2 * N], U8, name="w_cd", align_bytes=64)
+
+        def plane_start(a, u):
+            return (2 * (PASSES - 1 - a) + u) * T
+
+        nc.vector.memset(planes[:, 4 * PASSES * T :], 0.0)
+        nc.vector.memset(w_sc[:].rearrange("p g n -> p (g n)").bitcast(I32), 0)
+
+        order = [(a, u) for a in range(PASSES) for u in (1, 0)]
+        x_rows = xT.rearrange("(a p u j) t -> a u p j t", p=P, u=2, j=2)
+        offs_sb = lists.tile([P, S // 16], U16, name="offs_sb")
+        raw = {}
+        for i, (a, u) in enumerate(order):
+            raw[a, u] = keep.tile([P, 2, T], F32, name=f"raw{a}{u}")
+            nc.sync.dma_start(raw[a, u][:], x_rows[a, u])
+            if i == 0:
+                nc.sync.dma_start(offs_sb[:], offs)
+
+        sc_rows = w_scales.rearrange("e a (q r) n -> r q (e a) n", r=4)
+        for r in range(4):
+            nc.sync.dma_start(w_sc[r:P:32].bitcast(I32), sc_rows[r].bitcast(I32))
+        cd_rows = w_words.rearrange("e a p n -> p (e a) n")
+        for g0, g1 in ((0, 12), (12, 24), (24, 39)):
+            nc.sync.dma_start(w_cd[:, g0:g1, :].bitcast(I32), cd_rows[:, g0:g1, :].bitcast(I32))
+        bias = keep.tile([P, E + 1], F32, name="bias")
+        nc.sync.dma_start(bias[:], b)
+        pos_sb = []
+        for r, pos in enumerate((pos1, pos2, pos3)):
+            pos_sb.append(lists.tile([P, T // 16], U16, name=f"pos_sb{r}"))
+            nc.sync.dma_start(pos_sb[r][:], pos)
+        gate_sb = keep.tile([P, TOP, T], F32, name="gate_sb")
+        nc.sync.dma_start(gate_sb[:], gate.rearrange("r p t -> p r t"))
+
+        for i, (a, u) in enumerate(order):
+            c0 = 2 * plane_start(a, u)
+            dst = planes[:, c0 : c0 + 2 * T].rearrange("p (t j) -> p t j", j=2)
+            src = raw[a, u][:].rearrange("p j t -> p t j")
+            if i == 0:
+                nc.vector.tensor_copy(dst, src)
+            else:
+                nc.scalar.copy(dst, src)
+
+        def gather(a, s0, n, window):
+            got = keep.tile([P, 2, 2 * n], BF16, name=f"got{a}_{s0}", align_bytes=64)
+            for u in (1, 0):
+                w0 = plane_start(a, u)
+                nc.vector.tensor_copy(
+                    got[:, u, :].bitcast(U32),
+                    plane_words[:, w0 : w0 + window].indirect(offs_sb[:, s0 // 16 : (s0 + n) // 16]),
+                )
+            return got[:].bitcast(U32)
+
+        pairs = {}
+        first = gather(0, 0, S, 2048)
+        for c in range(CHUNKS):
+            pairs[0, c] = first[:, :, c * CH : (c + 1) * CH]
+        for c in range(CHUNKS):
+            for a in range(1, PASSES):
+                pairs[a, c] = gather(a, c * CH, CH, 1024)
+        for a in range(PASSES):
+            w0 = plane_start(a, 0)
+            pairs[a, CHUNKS] = plane_words[:, w0 : w0 + 2 * T].rearrange("p (u t) -> p u t", u=2)
+
+        steps = [(0, c) for c in range(CHUNKS)]
+        steps = steps + [(a, c) for c in range(CHUNKS) for a in range(1, PASSES)]
+        steps = steps + [(a, CHUNKS) for a in range(PASSES)]
+
+        woven = {}
+        for a, c in steps:
+            woven[a, c] = keep.tile([P, 4 * CH], BF16, name=f"woven{a}{c}", align_bytes=64)
+            nc.scalar.copy(
+                woven[a, c][:].bitcast(U32).rearrange("p (s u) -> p s u", u=2),
+                pairs[a, c].rearrange("p u s -> p s u"),
+            )
+
+        codes, scales = {}, {}
+        for a, c in steps:
+            codes[a, c] = keep.tile([P, CH], U32, name=f"codes{a}{c}", align_bytes=64)
+            scales[a, c] = keep.tile([P, CH], U8, name=f"scales{a}{c}", align_bytes=64)
+            nc.vector.quantize_mx(codes[a, c][:].bitcast(FP8X4), scales[a, c][:], woven[a, c][:])
+
+        def product(acc, e, a, c, cols):
+            g = e * PASSES + a
+            nc.tensor.matmul_mx(
+                acc,
+                lhsT=w_cd[:, g, :].bitcast(FP4X4),
+                lhsT_scale=w_sc[:, g, :],
+                rhs=codes[a, c][:, cols].bitcast(FP8X4),
+                rhs_scale=scales[a, c][:, cols],
+                start=(a == 0),
+                stop=(a == PASSES - 1),
+            )
+
+        per = CH // C
+        y = keep.tile([P, S], F32, name="y")
+        for c in range(CHUNKS - 1):
+            bank = psum.tile([P, CH], F32, name=f"bank{c}")
+            for i in range(per):
+                cols = slice(i * C, (i + 1) * C)
+                for a in range(PASSES):
+                    product(bank[:, cols], c * per + i, a, c, cols)
+            for i in range(per):
+                e = c * per + i
+                nc.scalar.activation(
+                    y[:, e * C : (e + 1) * C], bank[:, i * C : (i + 1) * C], RELU, bias=bias[:, e : e + 1]
+                )
+        c = CHUNKS - 1
+        last = [psum.tile([P, C], F32, name=f"last{i}") for i in range(per)]
+        for a in range(PASSES):
+            for i in range(per):
+                product(last[i][:], c * per + i, a, c, slice(i * C, (i + 1) * C))
+        for i in range(per):
+            e = c * per + i
+            nc.scalar.activation(y[:, e * C : (e + 1) * C], last[i][:], RELU, bias=bias[:, e : e + 1])
+
+        shared = psum.tile([P, T], F32, name="shared")
+        for a in range(PASSES):
+            product(shared[:], E, a, CHUNKS, slice(0, T))
+        ys = keep.tile([P, T], F32, name="ys")
+        nc.scalar.activation(ys[:], shared[:], RELU, bias=bias[:, E : E + 1])
+
+        terms = []
+        for r in range(TOP):
+            terms.append(keep.tile([P, T], F32, name=f"term{r}"))
+            nc.vector.tensor_tensor(terms[r][:], y[:].indirect(pos_sb[r][:]), gate_sb[:, r, :], MULT)
+        left = keep.tile([P, T], F32, name="left")
+        nc.vector.tensor_tensor(left[:], terms[0][:], terms[1][:], ADD)
+        halves = [slice(0, T // 2), slice(T // 2, T)]
+        right, total = [], []
+        for h, cols in enumerate(halves):
+            right.append(keep.tile([P, T // 2], F32, name=f"right{h}"))
+            nc.vector.tensor_tensor(right[h][:], terms[2][:, cols], ys[:, cols], ADD)
+        for h, cols in enumerate(halves):
+            total.append(keep.tile([P, T // 2], F32, name=f"total{h}"))
+            nc.vector.tensor_tensor(total[h][:], left[:, cols], right[h][:], ADD)
+            nc.sync.dma_start(out[:, cols], total[h][:])

@@ -1,6 +1,7 @@
 from contextlib import ExitStack
 
 import concourse.mybir as mybir
+from concourse.masks import make_identity
 
 K, T, E, C, N = 1536, 512, 12, 128, 128
 TOP = 3
@@ -16,6 +17,7 @@ U8 = mybir.dt.uint8
 FP8X4 = mybir.dt.float8_e4m3fn_x4
 FP4X4 = mybir.dt.float4_e2m1fn_x4
 RELU = mybir.ActivationFunctionType.Relu
+COPY = mybir.ActivationFunctionType.Copy
 MULT = mybir.AluOpType.mult
 ADD = mybir.AluOpType.add
 
@@ -23,7 +25,7 @@ P = 128
 PASSES = K // 512
 CH = 512
 CHUNKS = S // CH
-PAD = 1536
+PAD = 1024
 
 
 def tile_moe_shr_lin_relu_kernel(
@@ -43,17 +45,21 @@ def tile_moe_shr_lin_relu_kernel(
         def plane_start(a, u):
             return (2 * (PASSES - 1 - a) + u) * T
 
-        nc.vector.memset(planes[:, 4 * PASSES * T :], 0.0)
-        nc.vector.memset(w_sc[:].rearrange("p g n -> p (g n)").bitcast(I32), 0)
+        nc.vector.memset(plane_words[:, 2 * PASSES * T :], 0)
+        nc.gpsimd.memset(w_sc[:].rearrange("p g n -> p (g n)").bitcast(I32), 0)
+        ident = keep.tile([P, P], F32, name="ident")
+        make_identity(nc, ident[:])
 
         order = [(a, u) for a in range(PASSES) for u in (1, 0)]
         x_rows = xT.rearrange("(a p u j) t -> a u p j t", p=P, u=2, j=2)
         offs_sb = lists.tile([P, S // 16], U16, name="offs_sb")
-        raw = {}
-        for i, (a, u) in enumerate(order):
-            raw[a, u] = keep.tile([P, 2, T], F32, name=f"raw{a}{u}")
-            nc.sync.dma_start(raw[a, u][:], x_rows[a, u])
-            if i == 0:
+        halves = [slice(0, T // 2), slice(T // 2, T)]
+        loads = [(order[0], cols) for cols in halves] + [(au, slice(0, T)) for au in order[1:]]
+        raw = []
+        for i, ((a, u), cols) in enumerate(loads):
+            raw.append(keep.tile([P, 2, cols.stop - cols.start], F32, name=f"raw{i}", tag=f"raw{i}", align_bytes=64))
+            nc.sync.dma_start(raw[i][:], x_rows[a, u][:, :, cols])
+            if i == 1:
                 nc.sync.dma_start(offs_sb[:], offs)
 
         sc_rows = w_scales.rearrange("e a (q r) n -> r q (e a) n", r=4)
@@ -68,109 +74,193 @@ def tile_moe_shr_lin_relu_kernel(
         for r, pos in enumerate((pos1, pos2, pos3)):
             pos_sb.append(lists.tile([P, T // 16], U16, name=f"pos_sb{r}"))
             nc.sync.dma_start(pos_sb[r][:], pos)
-        gate_sb = keep.tile([P, TOP, T], F32, name="gate_sb")
-        nc.sync.dma_start(gate_sb[:], gate.rearrange("r p t -> p r t"))
+        gate_sb = [keep.tile([P, T], F32, name=f"gate_sb{r}") for r in range(TOP)]
+        for r in range(TOP):
+            nc.sync.dma_start(gate_sb[r][:], gate[r])
 
-        for i, (a, u) in enumerate(order):
+        singles = keep.tile([P, 2, T], BF16, name="singles", align_bytes=64)
+        for i in range(2):
+            nc.scalar.copy(singles[:, :, halves[i]], raw[i][:])
+        for i, ((a, u), cols) in enumerate(loads):
             c0 = 2 * plane_start(a, u)
-            dst = planes[:, c0 : c0 + 2 * T].rearrange("p (t j) -> p t j", j=2)
-            src = raw[a, u][:].rearrange("p j t -> p t j")
-            if i == 0:
+            dst = planes[:, c0 + 2 * cols.start : c0 + 2 * cols.stop].rearrange("p (t j) -> p t j", j=2)
+            src = raw[i][:].rearrange("p j t -> p t j")
+            if i < 2:
                 nc.vector.tensor_copy(dst, src)
             else:
                 nc.scalar.copy(dst, src)
 
-        def gather(a, s0, n, window):
-            got = keep.tile([P, 2, 2 * n], BF16, name=f"got{a}_{s0}", align_bytes=64)
-            for u in (1, 0):
+        pairs, woven, codes, scales = {}, {}, {}, {}
+
+        def gather(a, s0, n, tag, us=(1, 0)):
+            got = keep.tile([P, 2, 2 * n], BF16, name=f"got{a}_{s0}", tag=tag, align_bytes=64)
+            for u in us:
                 w0 = plane_start(a, u)
                 nc.vector.tensor_copy(
                     got[:, u, :].bitcast(U32),
-                    plane_words[:, w0 : w0 + window].indirect(offs_sb[:, s0 // 16 : (s0 + n) // 16]),
+                    plane_words[:, w0 : w0 + max(1024, n + 512)].indirect(offs_sb[:, s0 // 16 : (s0 + n) // 16]),
                 )
-            return got[:].bitcast(U32)
+            for m0 in range(0, n, CH):
+                pairs[a, s0 + m0] = got[:].bitcast(U32)[:, :, m0 : min(n, m0 + CH)]
+            return got
 
-        pairs = {}
-        first = gather(0, 0, S, 2048)
-        for c in range(CHUNKS):
-            pairs[0, c] = first[:, :, c * CH : (c + 1) * CH]
-        for c in range(CHUNKS):
-            for a in range(1, PASSES):
-                pairs[a, c] = gather(a, c * CH, CH, 1024)
-        for a in range(PASSES):
-            w0 = plane_start(a, 0)
-            pairs[a, CHUNKS] = plane_words[:, w0 : w0 + 2 * T].rearrange("p (u t) -> p u t", u=2)
-
-        steps = [(0, c) for c in range(CHUNKS)]
-        steps = steps + [(a, c) for c in range(CHUNKS) for a in range(1, PASSES)]
-        steps = steps + [(a, CHUNKS) for a in range(PASSES)]
-
-        woven = {}
-        for a, c in steps:
-            woven[a, c] = keep.tile([P, 4 * CH], BF16, name=f"woven{a}{c}", align_bytes=64)
-            nc.scalar.copy(
-                woven[a, c][:].bitcast(U32).rearrange("p (s u) -> p s u", u=2),
-                pairs[a, c].rearrange("p u s -> p s u"),
+        def gather_singles(got, s0, m0, n, j):
+            nc.scalar.activation(
+                got[:, 1, :].rearrange("p (s j) -> p s j", j=2)[:, m0 : m0 + n, j],
+                singles[:, j, :].indirect(offs_sb[:, (s0 + m0) // 16 : (s0 + m0 + n) // 16]),
+                COPY,
             )
 
-        codes, scales = {}, {}
-        for a, c in steps:
-            codes[a, c] = keep.tile([P, CH], U32, name=f"codes{a}{c}", align_bytes=64)
-            scales[a, c] = keep.tile([P, CH], U8, name=f"scales{a}{c}", align_bytes=64)
-            nc.vector.quantize_mx(codes[a, c][:].bitcast(FP8X4), scales[a, c][:], woven[a, c][:])
+        def weave(a, s0):
+            n = pairs[a, s0].shape[2]
+            if (a, s0) not in woven:
+                woven[a, s0] = keep.tile([P, 4 * n], BF16, name=f"woven{a}_{s0}", align_bytes=64)[:]
+            nc.scalar.copy(
+                woven[a, s0].bitcast(U32).rearrange("p (s u) -> p s u", u=2),
+                pairs[a, s0].rearrange("p u s -> p s u"),
+            )
 
-        def product(acc, e, a, c, cols):
+        def weave_shared(a, dst):
+            w0 = plane_start(a, 0)
+            nc.scalar.copy(
+                dst.bitcast(U32).rearrange("p (s u) -> p s u", u=2),
+                plane_words[:, w0 : w0 + 2 * T].rearrange("p (u t) -> p t u", u=2),
+            )
+
+        def quantize(src, name, tag):
+            n = src.shape[1] // 4
+            cd = keep.tile([P, n], U32, name=f"codes{name}", tag=tag, align_bytes=64)
+            sc = keep.tile([P, n], U8, name=f"scales{name}", align_bytes=64)
+            nc.vector.quantize_mx(cd[:].bitcast(FP8X4), sc[:], src)
+            return cd, sc
+
+        def quantize_slots(a, s0):
+            cd, sc = quantize(woven[a, s0], f"{a}_{s0}", f"codes{a}_{s0}")
+            for m0 in range(0, cd.shape[1], C):
+                codes[a, (s0 + m0) // C] = cd[:, m0 : m0 + C]
+                scales[a, (s0 + m0) // C] = sc[:, m0 : m0 + C]
+
+        def product(acc, e, a):
             g = e * PASSES + a
             nc.tensor.matmul_mx(
                 acc,
                 lhsT=w_cd[:, g, :].bitcast(FP4X4),
                 lhsT_scale=w_sc[:, g, :],
-                rhs=codes[a, c][:, cols].bitcast(FP8X4),
-                rhs_scale=scales[a, c][:, cols],
+                rhs=codes[a, e].bitcast(FP8X4),
+                rhs_scale=scales[a, e],
                 start=(a == 0),
                 stop=(a == PASSES - 1),
             )
 
-        per = CH // C
         y = keep.tile([P, S], F32, name="y")
-        for c in range(CHUNKS - 1):
-            bank = psum.tile([P, CH], F32, name=f"bank{c}")
-            for i in range(per):
-                cols = slice(i * C, (i + 1) * C)
+        sums = {}
+
+        def products(e0, tag):
+            bank = psum.tile([P, 4 * C], F32, name=tag, tag=tag)
+            for i in range(4):
+                sums[e0 + i] = bank[:, i * C : (i + 1) * C]
                 for a in range(PASSES):
-                    product(bank[:, cols], c * per + i, a, c, cols)
-            for i in range(per):
-                e = c * per + i
-                nc.scalar.activation(
-                    y[:, e * C : (e + 1) * C], bank[:, i * C : (i + 1) * C], RELU, bias=bias[:, e : e + 1]
-                )
-        c = CHUNKS - 1
-        last = [psum.tile([P, C], F32, name=f"last{i}") for i in range(per)]
-        for a in range(PASSES):
-            for i in range(per):
-                product(last[i][:], c * per + i, a, c, slice(i * C, (i + 1) * C))
-        for i in range(per):
-            e = c * per + i
-            nc.scalar.activation(y[:, e * C : (e + 1) * C], last[i][:], RELU, bias=bias[:, e : e + 1])
+                    product(sums[e0 + i], e0 + i, a)
+
+        def activate(experts):
+            for e in experts:
+                nc.scalar.activation(y[:, e * C : (e + 1) * C], sums[e], RELU, bias=bias[:, e : e + 1])
+
+        A, B, C0, D0 = 0, CH, 2 * CH, 2 * CH + CH // 2
+        woven_s0 = keep.tile([P, 4 * T], BF16, name="woven_s0", align_bytes=64)
+        woven_s12 = keep.tile([P, 8 * T], BF16, name="woven_s12", align_bytes=64)
+        for i in range(4):
+            sums[8 + i] = psum.tile([P, C], F32, name=f"last{i}", tag=f"last{i}")[:]
+
+        gather(0, A, 2 * CH, "got0")
+        gather(1, A, CH, "got1")
+        got = gather(0, C0, CH, f"raw{len(loads) - 2}", us=(0,))
+        gather(2, A, CH, "got2")
+        early = keep.tile([P, 3 * 4 * CH], BF16, name="early", tag=f"raw{len(loads) - 1}", align_bytes=64)
+        for i, (a, s0) in enumerate(((0, A), (0, B), (1, A))):
+            woven[a, s0] = early[:, i * 4 * CH : (i + 1) * 4 * CH]
+            weave(a, s0)
+        gather_singles(got, C0, 0, CH // 2, 0)
+        weave(2, A)
+        gather_singles(got, C0, 0, CH // 2, 1)
+        for j in range(2):
+            gather_singles(got, C0, CH // 2, CH // 2, j)
+        gather(1, B, CH, "got1")
+        for a, s0 in ((0, A), (0, B), (1, A)):
+            quantize_slots(a, s0)
+        gather(2, B, CH, "got2")
+        quantize_slots(2, A)
+        products(0, "bank0")
+        weave(1, B)
+        weave(0, C0)
+        weave_shared(0, woven_s0[:])
+        weave(2, B)
+        gather(1, C0, CH, "got1")
+        quantize_slots(1, B)
+        quantize_slots(0, C0)
+        for e in range(8, 12):
+            product(sums[e], e, 0)
+        gather(2, C0, CH // 2, "got2")
+        quantize_slots(2, B)
+        products(4, "bank1")
+        weave_shared(1, woven_s12[:, : 4 * T])
+        weave(1, C0)
+        activate(range(0, 4))
+        gather(2, D0, CH // 2, "got1")
+        quantize_slots(1, C0)
+        for e in range(8, 12):
+            product(sums[e], e, 1)
+        weave(2, C0)
+        weave_shared(2, woven_s12[:, 4 * T :])
+        weave(2, D0)
+        activate(range(4, 8))
+        quantize_slots(2, C0)
+        cd, sc = quantize(woven_s0[:], "s0", "got2")
+        codes[0, E], scales[0, E] = cd[:], sc[:]
+        quantize_slots(2, D0)
+        cd, sc = quantize(woven_s12[:], "s12", "got1")
+        for a in (1, 2):
+            codes[a, E], scales[a, E] = cd[:, (a - 1) * T : a * T], sc[:, (a - 1) * T : a * T]
+        for e in range(8, 12):
+            product(sums[e], e, 2)
+        activate(range(8, 12))
 
         shared = psum.tile([P, T], F32, name="shared")
         for a in range(PASSES):
-            product(shared[:], E, a, CHUNKS, slice(0, T))
+            product(shared[:], E, a)
         ys = keep.tile([P, T], F32, name="ys")
         nc.scalar.activation(ys[:], shared[:], RELU, bias=bias[:, E : E + 1])
 
-        terms = []
-        for r in range(TOP):
-            terms.append(keep.tile([P, T], F32, name=f"term{r}"))
-            nc.vector.tensor_tensor(terms[r][:], y[:].indirect(pos_sb[r][:]), gate_sb[:, r, :], MULT)
-        left = keep.tile([P, T], F32, name="left")
-        nc.vector.tensor_tensor(left[:], terms[0][:], terms[1][:], ADD)
-        halves = [slice(0, T // 2), slice(T // 2, T)]
-        right, total = [], []
+        def fetch(r, cols):
+            term = keep.tile([P, cols.stop - cols.start], F32, name=f"term{r}_{cols.start}")
+            nc.vector.tensor_tensor(
+                term[:], y[:].indirect(pos_sb[r][:, cols.start // 16 : cols.stop // 16]), gate_sb[r][:, cols], MULT
+            )
+            return term
+
+        term0 = fetch(0, slice(0, T))
+        term1 = [fetch(1, cols) for cols in halves]
+        term2 = fetch(2, slice(0, T))
+
+        def turn(blocks, tag):
+            acc = psum.tile([P, len(blocks) * P], F32, name=f"turned{blocks[0]}", tag=tag)
+            for i, j in enumerate(blocks):
+                cols = slice(j * P, (j + 1) * P)
+                parts = (term0[:, cols], ys[:, cols], term1[j // 2][:, (j % 2) * P : (j % 2 + 1) * P])
+                for m, part in enumerate(parts):
+                    nc.tensor.matmul(
+                        acc[:, i * P : (i + 1) * P], lhsT=part, rhs=ident[:],
+                        is_transpose=True, start=(m == 0), stop=(m == len(parts) - 1),
+                    )
+            turned = keep.tile([P, len(blocks) * P], F32, name=f"turned_sb{blocks[0]}")
+            nc.scalar.copy(turned[:], acc[:])
+            return [turned[:, i * P : (i + 1) * P] for i in range(len(blocks))]
+
+        turned = turn((0, 1), "bank0") + turn((2,), "bank1") + turn((3,), "last0")
         for h, cols in enumerate(halves):
-            right.append(keep.tile([P, T // 2], F32, name=f"right{h}"))
-            nc.vector.tensor_tensor(right[h][:], terms[2][:, cols], ys[:, cols], ADD)
-        for h, cols in enumerate(halves):
-            total.append(keep.tile([P, T // 2], F32, name=f"total{h}"))
-            nc.vector.tensor_tensor(total[h][:], left[:, cols], right[h][:], ADD)
-            nc.sync.dma_start(out[:, cols], total[h][:])
+            back = psum.tile([P, T // 2], F32, name=f"back{h}", tag=f"last{1 + h}")
+            for i in range(2):
+                nc.tensor.transpose(back[:, i * P : (i + 1) * P], turned[2 * h + i], ident[:])
+            total = keep.tile([P, T // 2], F32, name=f"total{h}")
+            nc.vector.tensor_tensor(total[:], back[:], term2[:, cols], ADD)
+            nc.sync.dma_start(out[:, cols], total[:])

@@ -46,7 +46,7 @@ def tile_moe_shr_lin_relu_kernel(
             return (2 * (PASSES - 1 - a) + u) * T
 
         nc.vector.memset(plane_words[:, 2 * PASSES * T :], 0)
-        nc.gpsimd.memset(w_sc[:].rearrange("p g n -> p (g n)").bitcast(I32), 0)
+        nc.vector.memset(w_sc[:].rearrange("p g n -> p (g n)").bitcast(I32), 0)
         ident = keep.tile([P, P], F32, name="ident")
         make_identity(nc, ident[:])
 
@@ -114,7 +114,7 @@ def tile_moe_shr_lin_relu_kernel(
         def weave(a, s0):
             n = pairs[a, s0].shape[2]
             if (a, s0) not in woven:
-                woven[a, s0] = keep.tile([P, 4 * n], BF16, name=f"woven{a}_{s0}", align_bytes=64)[:]
+                woven[a, s0] = keep.tile([P, 4 * n], BF16, name=f"woven{a}_{s0}", tag=f"woven{a}_{s0}", align_bytes=64)[:]
             nc.scalar.copy(
                 woven[a, s0].bitcast(U32).rearrange("p (s u) -> p s u", u=2),
                 pairs[a, s0].rearrange("p u s -> p s u"),
@@ -218,9 +218,9 @@ def tile_moe_shr_lin_relu_kernel(
         cd, sc = quantize(woven_s0[:], "s0", "got2")
         codes[0, E], scales[0, E] = cd[:], sc[:]
         quantize_slots(2, D0)
-        cd, sc = quantize(woven_s12[:], "s12", "got1")
-        for a in (1, 2):
-            codes[a, E], scales[a, E] = cd[:, (a - 1) * T : a * T], sc[:, (a - 1) * T : a * T]
+        for a, tag in ((1, "got1"), (2, f"woven2_{D0}")):
+            cd, sc = quantize(woven_s12[:, (a - 1) * 4 * T : a * 4 * T], f"s{a}", tag)
+            codes[a, E], scales[a, E] = cd[:], sc[:]
         for e in range(8, 12):
             product(sums[e], e, 2)
         activate(range(8, 12))
@@ -240,27 +240,30 @@ def tile_moe_shr_lin_relu_kernel(
 
         term0 = fetch(0, slice(0, T))
         term1 = [fetch(1, cols) for cols in halves]
-        term2 = fetch(2, slice(0, T))
+        term2 = [fetch(2, cols) for cols in halves]
 
-        def turn(blocks, tag):
-            acc = psum.tile([P, len(blocks) * P], F32, name=f"turned{blocks[0]}", tag=tag)
-            for i, j in enumerate(blocks):
-                cols = slice(j * P, (j + 1) * P)
-                parts = (term0[:, cols], ys[:, cols], term1[j // 2][:, (j % 2) * P : (j % 2 + 1) * P])
-                for m, part in enumerate(parts):
-                    nc.tensor.matmul(
-                        acc[:, i * P : (i + 1) * P], lhsT=part, rhs=ident[:],
-                        is_transpose=True, start=(m == 0), stop=(m == len(parts) - 1),
-                    )
-            turned = keep.tile([P, len(blocks) * P], F32, name=f"turned_sb{blocks[0]}")
-            nc.scalar.copy(turned[:], acc[:])
-            return [turned[:, i * P : (i + 1) * P] for i in range(len(blocks))]
-
-        turned = turn((0, 1), "bank0") + turn((2,), "bank1") + turn((3,), "last0")
+        blocks = T // P
+        tags = ("bank0", "bank1", "last0", "last1")
+        acc = [psum.tile([P, P], F32, name=f"acc{j}", tag=tags[j]) for j in range(blocks)]
+        parts = [
+            [term0[:, j * P : (j + 1) * P] for j in range(blocks)],
+            [ys[:, j * P : (j + 1) * P] for j in range(blocks)],
+            [term1[j // 2][:, (j % 2) * P : (j % 2 + 1) * P] for j in range(blocks)],
+        ]
+        for m in range(len(parts)):
+            for j in range(blocks):
+                nc.tensor.matmul(
+                    acc[j][:], lhsT=parts[m][j], rhs=ident[:],
+                    is_transpose=True, start=(m == 0), stop=(m == len(parts) - 1),
+                )
+        turned = []
+        for j in range(blocks):
+            turned.append(keep.tile([P, P], F32, name=f"turned{j}")[:])
+            nc.scalar.copy(turned[j], acc[j][:])
         for h, cols in enumerate(halves):
-            back = psum.tile([P, T // 2], F32, name=f"back{h}", tag=f"last{1 + h}")
+            back = psum.tile([P, T // 2], F32, name=f"back{h}", tag=f"last{2 + h}")
             for i in range(2):
                 nc.tensor.transpose(back[:, i * P : (i + 1) * P], turned[2 * h + i], ident[:])
             total = keep.tile([P, T // 2], F32, name=f"total{h}")
-            nc.vector.tensor_tensor(total[:], back[:], term2[:, cols], ADD)
+            nc.vector.tensor_tensor(total[:], back[:], term2[h][:], ADD)
             nc.sync.dma_start(out[:, cols], total[:])

from contextlib import ExitStack

import concourse.mybir as mybir
from concourse.masks import make_identity

K, T, E, C, N = 1536, 512, 12, 128, 128
TOP = 3
S = E * C
FLOPS = 2 * K * N * (S + T)

F32 = mybir.dt.float32
BF16 = mybir.dt.bfloat16
I32 = mybir.dt.int32
U32 = mybir.dt.uint32
U16 = mybir.dt.uint16
U8 = mybir.dt.uint8
FP8X4 = mybir.dt.float8_e4m3fn_x4
FP4X4 = mybir.dt.float4_e2m1fn_x4
RELU = mybir.ActivationFunctionType.Relu
COPY = mybir.ActivationFunctionType.Copy
MULT = mybir.AluOpType.mult
ADD = mybir.AluOpType.add

P = 128
PASSES = K // 512
CH = 512
CHUNKS = S // CH
PAD = 1024


def tile_moe_shr_lin_relu_kernel(
    tc, xT, w_words, w_scales, b, gate, offs, pos1, pos2, pos3, out
):
    nc = tc.nc
    with ExitStack() as ctx:
        lists = ctx.enter_context(tc.tile_pool(name="lists", bufs=1))
        keep = ctx.enter_context(tc.tile_pool(name="keep", bufs=1))
        psum = ctx.enter_context(tc.psum_pool(name="psum", bufs=1))

        planes = keep.tile([P, 2 * (2 * PASSES * T + PAD)], BF16, name="planes", align_bytes=64)
        plane_words = planes[:].bitcast(U32)
        w_sc = keep.tile([P, (E + 1) * PASSES, N], U8, name="w_sc", align_bytes=64)
        w_cd = keep.tile([P, (E + 1) * PASSES, 2 * N], U8, name="w_cd", align_bytes=64)

        def plane_start(a, u):
            return (2 * (PASSES - 1 - a) + u) * T

        nc.vector.memset(plane_words[:, 2 * PASSES * T :], 0)
        nc.vector.memset(w_sc[:].rearrange("p g n -> p (g n)").bitcast(I32), 0)
        ident = keep.tile([P, P], F32, name="ident")
        make_identity(nc, ident[:])

        order = [(a, u) for a in range(PASSES) for u in (1, 0)]
        x_rows = xT.rearrange("(a p u j) t -> a u p j t", p=P, u=2, j=2)
        offs_sb = lists.tile([P, S // 16], U16, name="offs_sb")
        halves = [slice(0, T // 2), slice(T // 2, T)]
        loads = [(order[0], cols) for cols in halves] + [(au, slice(0, T)) for au in order[1:]]
        raw = []
        for i, ((a, u), cols) in enumerate(loads):
            raw.append(keep.tile([P, 2, cols.stop - cols.start], F32, name=f"raw{i}", tag=f"raw{i}", align_bytes=64))
            nc.sync.dma_start(raw[i][:], x_rows[a, u][:, :, cols])
            if i == 1:
                nc.sync.dma_start(offs_sb[:], offs)

        sc_rows = w_scales.rearrange("e a (q r) n -> r q (e a) n", r=4)
        for r in range(4):
            nc.sync.dma_start(w_sc[r:P:32].bitcast(I32), sc_rows[r].bitcast(I32))
        cd_rows = w_words.rearrange("e a p n -> p (e a) n")
        for g0, g1 in ((0, 12), (12, 24), (24, 39)):
            nc.sync.dma_start(w_cd[:, g0:g1, :].bitcast(I32), cd_rows[:, g0:g1, :].bitcast(I32))
        bias = keep.tile([P, E + 1], F32, name="bias")
        nc.sync.dma_start(bias[:], b)
        pos_sb = []
        for r, pos in enumerate((pos1, pos2, pos3)):
            pos_sb.append(lists.tile([P, T // 16], U16, name=f"pos_sb{r}"))
            nc.sync.dma_start(pos_sb[r][:], pos)
        gate_sb = [keep.tile([P, T], F32, name=f"gate_sb{r}") for r in range(TOP)]
        for r in range(TOP):
            nc.sync.dma_start(gate_sb[r][:], gate[r])

        singles = keep.tile([P, 2, T], BF16, name="singles", align_bytes=64)
        for i in range(2):
            nc.scalar.copy(singles[:, :, halves[i]], raw[i][:])
        for i, ((a, u), cols) in enumerate(loads):
            c0 = 2 * plane_start(a, u)
            dst = planes[:, c0 + 2 * cols.start : c0 + 2 * cols.stop].rearrange("p (t j) -> p t j", j=2)
            src = raw[i][:].rearrange("p j t -> p t j")
            if i < 2:
                nc.vector.tensor_copy(dst, src)
            else:
                nc.scalar.copy(dst, src)

        pairs, woven, codes, scales = {}, {}, {}, {}

        def gather(a, s0, n, tag, us=(1, 0)):
            got = keep.tile([P, 2, 2 * n], BF16, name=f"got{a}_{s0}", tag=tag, align_bytes=64)
            for u in us:
                w0 = plane_start(a, u)
                nc.vector.tensor_copy(
                    got[:, u, :].bitcast(U32),
                    plane_words[:, w0 : w0 + max(1024, n + 512)].indirect(offs_sb[:, s0 // 16 : (s0 + n) // 16]),
                )
            for m0 in range(0, n, CH):
                pairs[a, s0 + m0] = got[:].bitcast(U32)[:, :, m0 : min(n, m0 + CH)]
            return got

        def gather_singles(got, s0, m0, n, j):
            nc.scalar.activation(
                got[:, 1, :].rearrange("p (s j) -> p s j", j=2)[:, m0 : m0 + n, j],
                singles[:, j, :].indirect(offs_sb[:, (s0 + m0) // 16 : (s0 + m0 + n) // 16]),
                COPY,
            )

        def weave(a, s0):
            n = pairs[a, s0].shape[2]
            if (a, s0) not in woven:
                woven[a, s0] = keep.tile([P, 4 * n], BF16, name=f"woven{a}_{s0}", tag=f"woven{a}_{s0}", align_bytes=64)[:]
            nc.scalar.copy(
                woven[a, s0].bitcast(U32).rearrange("p (s u) -> p s u", u=2),
                pairs[a, s0].rearrange("p u s -> p s u"),
            )

        def weave_shared(a, dst):
            w0 = plane_start(a, 0)
            nc.scalar.copy(
                dst.bitcast(U32).rearrange("p (s u) -> p s u", u=2),
                plane_words[:, w0 : w0 + 2 * T].rearrange("p (u t) -> p t u", u=2),
            )

        def quantize(src, name, tag):
            n = src.shape[1] // 4
            cd = keep.tile([P, n], U32, name=f"codes{name}", tag=tag, align_bytes=64)
            sc = keep.tile([P, n], U8, name=f"scales{name}", align_bytes=64)
            nc.vector.quantize_mx(cd[:].bitcast(FP8X4), sc[:], src)
            return cd, sc

        def quantize_slots(a, s0):
            cd, sc = quantize(woven[a, s0], f"{a}_{s0}", f"codes{a}_{s0}")
            for m0 in range(0, cd.shape[1], C):
                codes[a, (s0 + m0) // C] = cd[:, m0 : m0 + C]
                scales[a, (s0 + m0) // C] = sc[:, m0 : m0 + C]

        def product(acc, e, a):
            g = e * PASSES + a
            nc.tensor.matmul_mx(
                acc,
                lhsT=w_cd[:, g, :].bitcast(FP4X4),
                lhsT_scale=w_sc[:, g, :],
                rhs=codes[a, e].bitcast(FP8X4),
                rhs_scale=scales[a, e],
                start=(a == 0),
                stop=(a == PASSES - 1),
            )

        y = keep.tile([P, S], F32, name="y")
        sums = {}

        def products(e0, tag):
            bank = psum.tile([P, 4 * C], F32, name=tag, tag=tag)
            for i in range(4):
                sums[e0 + i] = bank[:, i * C : (i + 1) * C]
                for a in range(PASSES):
                    product(sums[e0 + i], e0 + i, a)

        def activate(experts):
            for e in experts:
                nc.scalar.activation(y[:, e * C : (e + 1) * C], sums[e], RELU, bias=bias[:, e : e + 1])

        A, B, C0, D0 = 0, CH, 2 * CH, 2 * CH + CH // 2
        woven_s0 = keep.tile([P, 4 * T], BF16, name="woven_s0", align_bytes=64)
        woven_s12 = keep.tile([P, 8 * T], BF16, name="woven_s12", align_bytes=64)
        for i in range(4):
            sums[8 + i] = psum.tile([P, C], F32, name=f"last{i}", tag=f"last{i}")[:]

        gather(0, A, 2 * CH, "got0")
        gather(1, A, CH, "got1")
        got = gather(0, C0, CH, f"raw{len(loads) - 2}", us=(0,))
        gather(2, A, CH, "got2")
        early = keep.tile([P, 3 * 4 * CH], BF16, name="early", tag=f"raw{len(loads) - 1}", align_bytes=64)
        for i, (a, s0) in enumerate(((0, A), (0, B), (1, A))):
            woven[a, s0] = early[:, i * 4 * CH : (i + 1) * 4 * CH]
            weave(a, s0)
        gather_singles(got, C0, 0, CH // 2, 0)
        weave(2, A)
        gather_singles(got, C0, 0, CH // 2, 1)
        for j in range(2):
            gather_singles(got, C0, CH // 2, CH // 2, j)
        gather(1, B, CH, "got1")
        for a, s0 in ((0, A), (0, B), (1, A)):
            quantize_slots(a, s0)
        gather(2, B, CH, "got2")
        quantize_slots(2, A)
        products(0, "bank0")
        weave(1, B)
        weave(0, C0)
        weave_shared(0, woven_s0[:])
        weave(2, B)
        gather(1, C0, CH, "got1")
        quantize_slots(1, B)
        quantize_slots(0, C0)
        for e in range(8, 12):
            product(sums[e], e, 0)
        gather(2, C0, CH // 2, "got2")
        quantize_slots(2, B)
        products(4, "bank1")
        weave_shared(1, woven_s12[:, : 4 * T])
        weave(1, C0)
        activate(range(0, 4))
        gather(2, D0, CH // 2, "got1")
        quantize_slots(1, C0)
        for e in range(8, 12):
            product(sums[e], e, 1)
        weave(2, C0)
        weave_shared(2, woven_s12[:, 4 * T :])
        weave(2, D0)
        activate(range(4, 8))
        quantize_slots(2, C0)
        cd, sc = quantize(woven_s0[:], "s0", "got2")
        codes[0, E], scales[0, E] = cd[:], sc[:]
        quantize_slots(2, D0)
        for a, tag in ((1, "got1"), (2, f"woven2_{D0}")):
            cd, sc = quantize(woven_s12[:, (a - 1) * 4 * T : a * 4 * T], f"s{a}", tag)
            codes[a, E], scales[a, E] = cd[:], sc[:]
        for e in range(8, 12):
            product(sums[e], e, 2)
        activate(range(8, 12))

        shared = psum.tile([P, T], F32, name="shared")
        for a in range(PASSES):
            product(shared[:], E, a)
        ys = keep.tile([P, T], F32, name="ys")
        nc.scalar.activation(ys[:], shared[:], RELU, bias=bias[:, E : E + 1])

        def fetch(r, cols):
            term = keep.tile([P, cols.stop - cols.start], F32, name=f"term{r}_{cols.start}")
            nc.vector.tensor_tensor(
                term[:], y[:].indirect(pos_sb[r][:, cols.start // 16 : cols.stop // 16]), gate_sb[r][:, cols], MULT
            )
            return term

        term0 = fetch(0, slice(0, T))
        term1 = [fetch(1, cols) for cols in halves]
        term2 = [fetch(2, cols) for cols in halves]

        blocks = T // P
        tags = ("bank0", "bank1", "last0", "last1")
        acc = [psum.tile([P, P], F32, name=f"acc{j}", tag=tags[j]) for j in range(blocks)]
        parts = [
            [term0[:, j * P : (j + 1) * P] for j in range(blocks)],
            [ys[:, j * P : (j + 1) * P] for j in range(blocks)],
            [term1[j // 2][:, (j % 2) * P : (j % 2 + 1) * P] for j in range(blocks)],
        ]
        for m in range(len(parts)):
            for j in range(blocks):
                nc.tensor.matmul(
                    acc[j][:], lhsT=parts[m][j], rhs=ident[:],
                    is_transpose=True, start=(m == 0), stop=(m == len(parts) - 1),
                )
        turned = []
        for j in range(blocks):
            turned.append(keep.tile([P, P], F32, name=f"turned{j}")[:])
            nc.scalar.copy(turned[j], acc[j][:])
        for h, cols in enumerate(halves):
            back = psum.tile([P, T // 2], F32, name=f"back{h}", tag=f"last{2 + h}")
            for i in range(2):
                nc.tensor.transpose(back[:, i * P : (i + 1) * P], turned[2 * h + i], ident[:])
            total = keep.tile([P, T // 2], F32, name=f"total{h}")
            nc.vector.tensor_tensor(total[:], back[:], term2[h][:], ADD)
            nc.sync.dma_start(out[:, cols], total[:])
